import numpy as np
import ml_dtypes


def mxq(x, axis, fmt="e4m3"):
    dtype, down = {"e4m3": (ml_dtypes.float8_e4m3fn, 7), "e5m2": (ml_dtypes.float8_e5m2, 14)}[fmt]
    v = np.moveaxis(np.asarray(x, np.float32).astype(ml_dtypes.bfloat16).astype(np.float64), axis, -1)
    blocks = v.reshape(v.shape[:-1] + (-1, 32))
    amax = np.abs(blocks).max(-1, keepdims=True)
    byte = np.maximum(np.where(amax > 0, np.frexp(amax)[1] - 1 + 127, 0) - down, 1)
    scale = np.exp2(byte - 127.0)
    codes = (blocks / scale).astype(np.float32).astype(dtype).astype(np.float64)
    return np.moveaxis((codes * scale).reshape(v.shape), -1, axis)


WIDE = False


def mx_kscale(k, group=512):
    if not WIDE:
        return np.ones(k)
    levels = np.array([10, -10, 5, -5, 0])
    if group != 512:
        return np.exp2(np.random.permutation(np.resize(levels, k // group))).repeat(group)
    if k % 512:
        return np.exp2(np.random.permutation(np.resize(levels, k // 32))).repeat(32)
    a = np.empty((k // 512, 16))
    for p in range(k // 512):
        a[p, :8] = np.random.permutation(np.resize(levels, 8))
        for g in range(8):
            far = levels[np.abs(levels - a[p, g]) >= 10]
            a[p, g + 8] = far[np.random.randint(len(far))]
    return np.exp2(a.ravel()).repeat(32)


def f64(x):
    return np.asarray(x).astype(np.float64)


def striped(idx):
    return np.tile(np.asarray(idx).reshape(-1, 16).T, (8, 1)).astype(np.uint16)


def unstriped(offs):
    return offs[:16].T.reshape(-1).astype(np.int64)


H, KV, D, NQ, N = 4, 4, 256, 512, 512
CAP = 2.0


def setup_inputs():
    n = np.random.standard_normal
    s = mx_kscale(D, 0)[:, None]
    u = mx_kscale(N)
    t = np.random.uniform(0.5, 2.0, N) * u
    v = n((KV, N, 128))
    v[:, :, 127] = 1.0
    return {
        "qT": (n((H, D, NQ)) * s * (0.70 / np.sqrt(D))).astype(np.float32),
        "kT": (n((KV, D, N)) / s).astype(np.float32),
        "t": t.reshape(N, 1).astype(np.float32),
        "v": (v / t[:, None]).astype(np.float32),
        "og": n((H, NQ, 128)).astype(np.float32),
    }


def reference(qT, kT, t, v, og):
    a = mxq(f64(kT), 1, "e4m3").transpose(0, 2, 1) @ mxq(f64(qT), 1, "e4m3")
    a = CAP * np.tanh(a / CAP)
    p = np.square(np.maximum(a, 0.0))
    w = p * f64(t)
    y = mxq(w, 1, "e4m3").transpose(0, 2, 1) @ mxq(f64(v), 1, "e4m3")
    y = y / (y[:, :, 127:128] + 1.0)
    y = y / (1.0 + np.exp(-f64(og)))
    return y

@@ -1,0 +1,261 @@
+from contextlib import ExitStack
+
+import concourse.mybir as mybir
+
+H, D, NQ, N, E = 4, 256, 512, 512, 128
+CAP = 2.0
+FLOPS = 2 * H * NQ * N * (D + E)
+
+F32 = mybir.dt.float32
+BF16 = mybir.dt.bfloat16
+U32 = mybir.dt.uint32
+U8 = mybir.dt.uint8
+FP8X4 = mybir.dt.float8_e4m3fn_x4
+ALU = mybir.AluOpType
+ACT = mybir.ActivationFunctionType
+
+P = 128
+PACK = 4
+ROWS = 64
+QT = 128
+TILES = NQ // QT
+UNITS = (H // 2) * TILES
+SCORE_BANKS = 2
+Y_BANKS = 4
+SQUARE_ON_VECTOR = ()
+Q_COPY_ON_SCALAR = ()
+ORDER = "lk:0 lk:1 lq:0 lo:0 lt: lq:1 lq:2 lk:2 lk:3 lq:3 lv:0 lo:1 lo:2 lq:4 lo:3 lo:4 lv:1 lo:5 lo:6 lo:7 lo:8 ck:0 ck:1 cq:0 qk:0 qq:0 sc:00 sc:01 sig:0 root: sign:0 cq:1 sign:1 qq:1 sc:10 sc:11 cap:00 cap:01 cq:2 cap:10 cap:11 rs:00 rs:01 rs:02 rs:03 qq:2 sc:20 sc:21 sc:30 sc:31 sq:0 ck:2 cap:20 cap:21 rs:10 rs:11 rs:12 rs:13 sq:1 qw:0 ck:3 cap:30 cap:31 rs:20 rs:21 rs:22 rs:23 sq:2 qk:1 cq:3 qw:1 qq:3 sc:40 sc:41 sc:50 sc:51 cap:40 cap:41 rs:30 rs:31 rs:32 rs:33 sq:3 sig:1 sig:2 cv:0 cv:1 qw:2 qv:0 val:0 val:1 val:2 cq:4 cap:50 cap:51 rs:40 rs:41 rs:42 rs:43 sq:4 sig:3 sig:4 qq:4 sc:60 sc:61 da:0 qw:3 val:3 sc:70 sc:71 dr:0 da:1 cv:2 dr:1 fin:00 fin:01 st:0 fin:10 fin:11 st:1 cap:60 cap:61 rs:50 rs:51 rs:52 rs:53 sq:5 da:2 cv:3 dr:2 qw:4 da:3 qv:1 dr:3 val:4 fin:20 fin:21 st:2 fin:30 fin:31 st:3 cap:70 cap:71 rs:60 rs:61 rs:62 rs:63 sq:6 sig:5 sig:6 da:4 qw:5 val:5 dr:4 rs:70 rs:71 rs:72 rs:73 sq:7 sig:7 sig:8 da:5 fin:40 fin:41 st:4 dr:5 qw:6 val:6 fin:50 fin:51 st:5 da:6 qw:7 val:7 dr:6 fin:60 fin:61 st:6 da:7 dr:7 fin:70 fin:71 st:7".split(" ")
+
+
+def tile_rows_a_relu2_cap_gate_kernel(tc, qT, kT, t, v, og, out):
+    nc = tc.nc
+    q_rows = qT.rearrange("h (p j) n -> (h p) j n", j=PACK)
+    k_rows = kT.rearrange("h (p j) n -> (h p) j n", j=PACK)
+
+    with ExitStack() as ctx:
+        sb = ctx.enter_context(tc.tile_pool(name="sb", bufs=1))
+        ps = ctx.enter_context(tc.psum_pool(name="ps", bufs=1))
+
+        def tiles(name, count, shape, dtype):
+            return [sb.tile(shape, dtype, name=name + str(i), align_bytes=64) for i in range(count)]
+
+        score = [
+            [ps.tile([P, PACK, QT], F32, name="score%d_%d" % (a, b)) for b in range(SCORE_BANKS)]
+            for a in range(2)
+        ]
+        y_ps = [ps.tile([P, PACK, E], F32, name="y%d" % b) for b in range(Y_BANKS)]
+
+        t_sb = sb.tile([P, PACK], F32, name="t_sb")
+        t_pos = sb.tile([P, PACK], F32, name="t_pos")
+        t_sign = sb.tile([P, PACK], F32, name="t_sign")
+        t_abs = sb.tile([P, PACK], F32, name="t_abs")
+        half = sb.tile([P, PACK], F32, name="half")
+        t_root = sb.tile([P, PACK], F32, name="t_root")
+
+        k_raw = tiles("k_raw", 4, [P, PACK, N // 2], F32)
+        k_bf = tiles("k_bf", 2, [P, PACK, P, PACK], BF16)
+        k_codes = tiles("k_codes", 2, [P, N], U32)
+        k_scales = tiles("k_scales", 2, [P, N], U8)
+
+        q_loads = [(0, 0, 1), (0, 1, 2), (0, 2, 4), (1, 0, 2), (1, 2, 4)]
+        q_raw = [
+            sb.tile([P, PACK, (b - a) * QT], F32, name="q_raw%d" % i) for i, (g, a, b) in enumerate(q_loads)
+        ]
+        q_bf = [sb.tile([P, (b - a) * QT, PACK], BF16, name="q_bf%d" % i, align_bytes=64) for i, (g, a, b) in enumerate(q_loads)]
+        q_codes = [sb.tile([P, (b - a) * QT], U32, name="q_codes%d" % i, align_bytes=64) for i, (g, a, b) in enumerate(q_loads)]
+        q_scales = [sb.tile([P, (b - a) * QT], U8, name="q_scales%d" % i, align_bytes=64) for i, (g, a, b) in enumerate(q_loads)]
+
+        v_raw = tiles("v_raw", 2, [P, 2, PACK, E], F32)
+        v_bf = tiles("v_bf", 2, [P, 2, E, PACK], BF16)
+        v_codes = tiles("v_codes", 2, [P, 2 * E], U32)
+        v_scales = tiles("v_scales", 2, [P, 2 * E], U8)
+
+        og_loads = [(0, 0, 1), (1, 0, 2), (0, 1, 2), (0, 2, 4), (1, 2, 4), (2, 0, 2), (3, 0, 2), (2, 2, 4), (3, 2, 4)]
+        og_raw = [
+            sb.tile([P, b - a, E], F32, name="og_raw%d" % i) for i, (h, a, b) in enumerate(og_loads)
+        ]
+        gate = [sb.tile([P, b - a, E], F32, name="gate%d" % i) for i, (h, a, b) in enumerate(og_loads)]
+
+        th = tiles("th", UNITS, [P, PACK, 2 * QT], F32)
+        root_w = tiles("root_w", UNITS, [P, PACK, 2 * QT], F32)
+        w_bf = tiles("w_bf", UNITS, [P, 2 * QT, PACK], BF16)
+        w_codes = tiles("w_codes", UNITS, [P, 2 * QT], U32)
+        w_scales = tiles("w_scales", UNITS, [P, 2 * QT], U8)
+        den = tiles("den", UNITS, [P, 2, 1], F32)
+        rden = tiles("rden", UNITS, [P, 2], F32)
+        res = tiles("res", UNITS, [P, 2, E], F32)
+
+        def load_k(i):
+            g, c = divmod(i, 2)
+            nc.sync.dma_start(out=k_raw[i][:], in_=k_rows[g * P : (g + 1) * P, :, c * 256 : (c + 1) * 256])
+
+        def load_q(i):
+            g, a, b = q_loads[i]
+            nc.sync.dma_start(out=q_raw[i][:], in_=q_rows[g * P : (g + 1) * P, :, a * QT : b * QT])
+
+        def load_v(g):
+            nc.sync.dma_start(
+                out=v_raw[g][:].rearrange("p h j e -> p h (j e)"),
+                in_=v[2 * g : 2 * g + 2].rearrange("h (p j) e -> p h (j e)", j=PACK),
+            )
+
+        def load_og(i):
+            h, a, b = og_loads[i]
+            nc.sync.dma_start(out=og_raw[i][:], in_=og[h, a * QT : b * QT, :].rearrange("(m p) e -> p m e", p=P))
+
+        def sigmoid(i):
+            nc.scalar.activation(out=gate[i][:], in_=og_raw[i][:], func=ACT.Sigmoid)
+
+        def gate_of(h, m):
+            i = [n for n, (hh, a, b) in enumerate(og_loads) if hh == h and a <= m < b][0]
+            return gate[i][:, m - og_loads[i][1], :]
+
+        def quantize(codes, scales, src):
+            nc.vector.quantize_mx(out=codes[:].bitcast(FP8X4), scales=scales[:], in_=src)
+
+        def copy_k(i):
+            g, c = divmod(i, 2)
+            nc.vector.tensor_copy(
+                out=k_bf[g][:, :, c * 64 : (c + 1) * 64, :].rearrange("p r s j -> p s j r"),
+                in_=k_raw[i][:].rearrange("p j (s r) -> p s j r", r=PACK),
+            )
+
+        def quant_k(g):
+            quantize(k_codes[g], k_scales[g], k_bf[g][:].rearrange("p r s j -> p (r s j)"))
+
+        def copy_q(i):
+            copy = nc.scalar.copy if i in Q_COPY_ON_SCALAR else nc.vector.tensor_copy
+            copy(
+                out=q_bf[i][:].rearrange("p (c i) j -> p c j i", i=2),
+                in_=q_raw[i][:].rearrange("p j (c i) -> p c j i", i=2),
+            )
+
+        def quant_q(i):
+            quantize(q_codes[i], q_scales[i], q_bf[i][:].rearrange("p c j -> p (c j)"))
+
+        def copy_v(h):
+            g, a = divmod(h, 2)
+            nc.vector.tensor_tensor(
+                out=v_bf[g][:, a].rearrange("p (c i) j -> p c j i", i=2),
+                in0=v_raw[g][:, a].rearrange("p j (c i) -> p c j i", i=2),
+                in1=t_sign[:].unsqueeze(1).unsqueeze(3).to_broadcast([P, E // 2, PACK, 2]),
+                op=ALU.mult,
+            )
+
+        def quant_v(g):
+            quantize(v_codes[g], v_scales[g], v_bf[g][:].rearrange("p h e j -> p (h e j)"))
+
+        def scores(u, a):
+            g, m = divmod(u, TILES)
+            i = [n for n, (gg, lo, hi) in enumerate(q_loads) if gg == g and lo <= m < hi][0]
+            q_cols = slice((m - q_loads[i][1]) * QT, (m - q_loads[i][1] + 1) * QT)
+            rows = slice(a * ROWS, (a + 1) * ROWS)
+            for r in range(PACK):
+                cols = slice(r * P, (r + 1) * P)
+                nc.tensor.matmul_mx(
+                    out=score[a][u % SCORE_BANKS][:, r, :],
+                    lhsT=k_codes[g][rows, cols].bitcast(FP8X4),
+                    lhsT_scale=k_scales[g][rows, cols],
+                    rhs=q_codes[i][rows, q_cols].bitcast(FP8X4),
+                    rhs_scale=q_scales[i][rows, q_cols],
+                    start=True,
+                    stop=True,
+                )
+
+        def cap(u, a):
+            nc.scalar.activation(
+                out=th[u][:, :, a * QT : (a + 1) * QT],
+                in_=score[a][u % SCORE_BANKS][:],
+                func=ACT.Tanh,
+                scale=1.0 / CAP,
+            )
+
+        def relu_scale(u, r):
+            nc.vector.tensor_scalar(
+                out=root_w[u][:, r, :],
+                in0=th[u][:, r, :],
+                scalar1=0.0,
+                scalar2=t_root[:, r : r + 1],
+                op0=ALU.max,
+                op1=ALU.mult,
+            )
+
+        def square(u):
+            src = root_w[u][:].rearrange("p r (c i) -> p c r i", i=2)
+            dst = w_bf[u][:].rearrange("p (c i) r -> p c r i", i=2)
+            if u in SQUARE_ON_VECTOR:
+                nc.vector.tensor_tensor(out=dst, in0=src, in1=src, op=ALU.mult)
+            else:
+                nc.scalar.activation(out=dst, in_=src, func=ACT.Square)
+
+        def quant_w(u):
+            quantize(w_codes[u], w_scales[u], w_bf[u][:].rearrange("p c r -> p (c r)"))
+
+        def y_of(u):
+            b, s = u % Y_BANKS, 2 * ((u // Y_BANKS) % 2)
+            return y_ps[b][:, s : s + 2, :]
+
+        def values(u):
+            g = u // TILES
+            for a in range(2):
+                cols = slice(a * P, (a + 1) * P)
+                nc.tensor.matmul_mx(
+                    out=y_of(u)[:, a, :],
+                    lhsT=w_codes[u][:, cols].bitcast(FP8X4),
+                    lhsT_scale=w_scales[u][:, cols],
+                    rhs=v_codes[g][:, cols].bitcast(FP8X4),
+                    rhs_scale=v_scales[g][:, cols],
+                    start=True,
+                    stop=True,
+                )
+
+        def den_add(u):
+            nc.vector.tensor_scalar(
+                out=den[u][:], in0=y_of(u)[:, :, E - 1 : E], scalar1=1.0, scalar2=None, op0=ALU.add
+            )
+
+        def den_recip(u):
+            nc.vector.reciprocal(out=rden[u][:], in_=den[u][:].rearrange("p a o -> p (a o)"))
+
+        def finish(u, a):
+            g, m = divmod(u, TILES)
+            nc.vector.scalar_tensor_tensor(
+                out=res[u][:, a, :],
+                in0=y_of(u)[:, a, :],
+                scalar=rden[u][:, a : a + 1],
+                in1=gate_of(2 * g + a, m),
+                op0=ALU.mult,
+                op1=ALU.mult,
+            )
+
+        def store(u):
+            g, m = divmod(u, TILES)
+            nc.sync.dma_start(
+                out=out[2 * g : 2 * g + 2, m * QT : (m + 1) * QT, :].rearrange("h p e -> p h e"),
+                in_=res[u][:],
+            )
+
+        def load_t():
+            nc.sync.dma_start(out=t_sb[:], in_=t.rearrange("(p j) o -> p (j o)", j=PACK))
+
+        def root():
+            nc.gpsimd.memset(half[:], 0.5)
+            nc.scalar.activation(out=t_abs[:], in_=t_sb[:], func=ACT.Abs, scale=CAP * CAP)
+            nc.gpsimd.tensor_tensor(out=t_root[:], in0=t_abs[:], in1=half[:], op=ALU.pow)
+
+        def sign(step):
+            if step == 0:
+                nc.vector.tensor_scalar(out=t_pos[:], in0=t_sb[:], scalar1=0.0, scalar2=2.0, op0=ALU.is_ge, op1=ALU.mult)
+            else:
+                nc.vector.tensor_scalar(out=t_sign[:], in0=t_pos[:], scalar1=-1.0, scalar2=None, op0=ALU.add)
+
+        steps = {
+            "lk": load_k, "lq": load_q, "lv": load_v, "lo": load_og, "lt": load_t, "root": root, "sign": sign,
+            "sig": sigmoid, "ck": copy_k, "qk": quant_k, "cq": copy_q, "qq": quant_q, "cv": copy_v, "qv": quant_v,
+            "sc": scores, "cap": cap, "rs": relu_scale, "sq": square, "qw": quant_w, "val": values,
+            "da": den_add, "dr": den_recip, "fin": finish, "st": store,
+        }
+        with tc.manual_schedule():
+            for word in ORDER:
+                parts = word.split(":")
+                steps[parts[0]](*[int(c) for c in parts[1]])

@@ -19,12 +19,13 @@ PACK = 4
 ROWS = 64
 QT = 128
 TILES = NQ // QT
-UNITS = (H // 2) * TILES
 SCORE_BANKS = 2
 Y_BANKS = 4
-SQUARE_ON_VECTOR = ()
-Q_COPY_ON_SCALAR = ()
-ORDER = "lk:0 lk:1 lq:0 lo:0 lt: lq:1 lq:2 lk:2 lk:3 lq:3 lv:0 lo:1 lo:2 lq:4 lo:3 lo:4 lv:1 lo:5 lo:6 lo:7 lo:8 ck:0 ck:1 cq:0 qk:0 qq:0 sc:00 sc:01 sig:0 root: sign:0 cq:1 sign:1 qq:1 sc:10 sc:11 cap:00 cap:01 cq:2 cap:10 cap:11 rs:00 rs:01 rs:02 rs:03 qq:2 sc:20 sc:21 sc:30 sc:31 sq:0 ck:2 cap:20 cap:21 rs:10 rs:11 rs:12 rs:13 sq:1 qw:0 ck:3 cap:30 cap:31 rs:20 rs:21 rs:22 rs:23 sq:2 qk:1 cq:3 qw:1 qq:3 sc:40 sc:41 sc:50 sc:51 cap:40 cap:41 rs:30 rs:31 rs:32 rs:33 sq:3 sig:1 sig:2 cv:0 cv:1 qw:2 qv:0 val:0 val:1 val:2 cq:4 cap:50 cap:51 rs:40 rs:41 rs:42 rs:43 sq:4 sig:3 sig:4 qq:4 sc:60 sc:61 da:0 qw:3 val:3 sc:70 sc:71 dr:0 da:1 cv:2 dr:1 fin:00 fin:01 st:0 fin:10 fin:11 st:1 cap:60 cap:61 rs:50 rs:51 rs:52 rs:53 sq:5 da:2 cv:3 dr:2 qw:4 da:3 qv:1 dr:3 val:4 fin:20 fin:21 st:2 fin:30 fin:31 st:3 cap:70 cap:71 rs:60 rs:61 rs:62 rs:63 sq:6 sig:5 sig:6 da:4 qw:5 val:5 dr:4 rs:70 rs:71 rs:72 rs:73 sq:7 sig:7 sig:8 da:5 fin:40 fin:41 st:4 dr:5 qw:6 val:6 fin:50 fin:51 st:5 da:6 qw:7 val:7 dr:6 fin:60 fin:61 st:6 da:7 dr:7 fin:70 fin:71 st:7".split(" ")
+GROUPS = [(0, 0, 1), (0, 1, 2), (0, 2, 4), (1, 0, 2), (1, 2, 3), (1, 3, 4)]
+Q_LOADS = [(0, 0, 1), (0, 1, 2), (0, 2, 4), (1, 0, 2), (1, 2, 4)]
+OG_LOADS = [(0, 2, 0, 1), (0, 2, 1, 2), (0, 1, 2, 4), (1, 2, 2, 4), (2, 3, 0, 2), (3, 4, 0, 2), (2, 4, 2, 3), (2, 4, 3, 4)]
+K_SPLIT = 88
+ORDER = "lk:0 lq:0 lt: lq:1 lq:2 lk:1 lq:3 lq:4 lv:0 lo:0 lo:1 lv:1 lo:2 lo:3 lo:4 lo:5 lo:6 lo:7 half: ck:00 ck:01 cq:01 root: qk:0 qq:0 sc:00 sc:01 cq:11 sign:0 qq:1 sc:10 sc:11 cap:00 cap:01 cq:20 sign:1 cap:10 cap:11 rs:00 rs:01 qq:2 rs:02 rs:03 sc:20 sc:21 sc:22 sc:23 sq:0021 rs:10 rs:11 rs:12 rs:13 ck:12 ck:13 cq:30 qk:1 qq:3 cap:20 cap:21 cap:22 cap:23 sq:1021 sc:30 sc:31 sc:32 sc:33 cq:40 rs:20 rs:21 qq:4 cv:0 rs:22 rs:23 cv:1 qw:002 qv:0 qw:102 cap:30 cap:31 cap:32 cap:33 sc:40 sc:41 val:002 val:102 sc:50 sc:51 sq:2021 sq:2241 sig:0 cv:2 da:0 da:1 rs:30 dr:0 dr:1 rs:31 rs:32 rs:33 qw:204 val:204 cap:40 cap:41 cap:50 cap:51 sig:1 cv:3 rs:40 rs:41 rs:42 rs:43 da:2 fin:00 fin:01 st:002 dr:2 sq:4020 sq:3021 sq:3241 sig:2 sig:3 rs:50 rs:51 rs:52 rs:53 qv:1 qw:402 val:402 fin:10 fin:11 st:102 qw:304 val:304 sq:5021 sig:4 sig:5 sig:6 sig:7 da:4 fin:20 fin:21 st:202 da:3 dr:4 fin:22 fin:23 st:224 dr:3 qw:502 val:502 fin:30 fin:31 st:302 fin:32 da:5 fin:33 st:324 dr:5 fin:40 fin:41 st:402 fin:50 fin:51 st:502".split(" ")
 
 
 def tile_rows_a_relu2_cap_gate_kernel(tc, qT, kT, t, v, og, out):
@@ -36,8 +37,8 @@ def tile_rows_a_relu2_cap_gate_kernel(tc, qT, kT, t, v, og, out):
         sb = ctx.enter_context(tc.tile_pool(name="sb", bufs=1))
         ps = ctx.enter_context(tc.psum_pool(name="ps", bufs=1))
 
-        def tiles(name, count, shape, dtype):
-            return [sb.tile(shape, dtype, name=name + str(i), align_bytes=64) for i in range(count)]
+        def tiles(name, shapes, dtype):
+            return [sb.tile(shape, dtype, name=name + str(i), align_bytes=64) for i, shape in enumerate(shapes)]
 
         score = [
             [ps.tile([P, PACK, QT], F32, name="score%d_%d" % (a, b)) for b in range(SCORE_BANKS)]
@@ -49,49 +50,50 @@ def tile_rows_a_relu2_cap_gate_kernel(tc, qT, kT, t, v, og, out):
         t_pos = sb.tile([P, PACK], F32, name="t_pos")
         t_sign = sb.tile([P, PACK], F32, name="t_sign")
         t_abs = sb.tile([P, PACK], F32, name="t_abs")
+        zero = sb.tile([P, PACK], F32, name="zero")
         half = sb.tile([P, PACK], F32, name="half")
         t_root = sb.tile([P, PACK], F32, name="t_root")
 
-        k_raw = tiles("k_raw", 4, [P, PACK, N // 2], F32)
-        k_bf = tiles("k_bf", 2, [P, PACK, P, PACK], BF16)
-        k_codes = tiles("k_codes", 2, [P, N], U32)
-        k_scales = tiles("k_scales", 2, [P, N], U8)
+        k_raw = tiles("k_raw", [[P, PACK, N]] * 2, F32)
+        k_bf = tiles("k_bf", [[P, PACK, P, PACK]] * 2, BF16)
+        k_codes = tiles("k_codes", [[P, N]] * 2, U32)
+        k_scales = tiles("k_scales", [[P, N]] * 2, U8)
 
-        q_loads = [(0, 0, 1), (0, 1, 2), (0, 2, 4), (1, 0, 2), (1, 2, 4)]
-        q_raw = [
-            sb.tile([P, PACK, (b - a) * QT], F32, name="q_raw%d" % i) for i, (g, a, b) in enumerate(q_loads)
-        ]
-        q_bf = [sb.tile([P, (b - a) * QT, PACK], BF16, name="q_bf%d" % i, align_bytes=64) for i, (g, a, b) in enumerate(q_loads)]
-        q_codes = [sb.tile([P, (b - a) * QT], U32, name="q_codes%d" % i, align_bytes=64) for i, (g, a, b) in enumerate(q_loads)]
-        q_scales = [sb.tile([P, (b - a) * QT], U8, name="q_scales%d" % i, align_bytes=64) for i, (g, a, b) in enumerate(q_loads)]
+        q_width = [(hi - lo) * QT for g, lo, hi in Q_LOADS]
+        q_raw = tiles("q_raw", [[P, PACK, n] for n in q_width], F32)
+        q_bf = tiles("q_bf", [[P, n, PACK] for n in q_width], BF16)
+        q_codes = tiles("q_codes", [[P, n] for n in q_width], U32)
+        q_scales = tiles("q_scales", [[P, n] for n in q_width], U8)
 
-        v_raw = tiles("v_raw", 2, [P, 2, PACK, E], F32)
-        v_bf = tiles("v_bf", 2, [P, 2, E, PACK], BF16)
-        v_codes = tiles("v_codes", 2, [P, 2 * E], U32)
-        v_scales = tiles("v_scales", 2, [P, 2 * E], U8)
+        v_raw = tiles("v_raw", [[P, 2, PACK, E]] * 2, F32)
+        v_bf = tiles("v_bf", [[P, 2, E, PACK]] * 2, BF16)
+        v_codes = tiles("v_codes", [[P, 2 * E]] * 2, U32)
+        v_scales = tiles("v_scales", [[P, 2 * E]] * 2, U8)
 
-        og_loads = [(0, 0, 1), (1, 0, 2), (0, 1, 2), (0, 2, 4), (1, 2, 4), (2, 0, 2), (3, 0, 2), (2, 2, 4), (3, 2, 4)]
-        og_raw = [
-            sb.tile([P, b - a, E], F32, name="og_raw%d" % i) for i, (h, a, b) in enumerate(og_loads)
-        ]
-        gate = [sb.tile([P, b - a, E], F32, name="gate%d" % i) for i, (h, a, b) in enumerate(og_loads)]
+        og_shape = [[P, (h1 - h0) * (m1 - m0), E] for h0, h1, m0, m1 in OG_LOADS]
+        og_raw = tiles("og_raw", og_shape, F32)
+        gate = tiles("gate", og_shape, F32)
 
-        th = tiles("th", UNITS, [P, PACK, 2 * QT], F32)
-        root_w = tiles("root_w", UNITS, [P, PACK, 2 * QT], F32)
-        w_bf = tiles("w_bf", UNITS, [P, 2 * QT, PACK], BF16)
-        w_codes = tiles("w_codes", UNITS, [P, 2 * QT], U32)
-        w_scales = tiles("w_scales", UNITS, [P, 2 * QT], U8)
-        den = tiles("den", UNITS, [P, 2, 1], F32)
-        rden = tiles("rden", UNITS, [P, 2], F32)
-        res = tiles("res", UNITS, [P, 2, E], F32)
+        slots = [2 * (hi - lo) for g, lo, hi in GROUPS]
+        th = tiles("th", [[P, PACK, n * QT] for n in slots], F32)
+        root_w = tiles("root_w", [[P, PACK, n * QT] for n in slots], F32)
+        w_bf = tiles("w_bf", [[P, n * QT, PACK] for n in slots], BF16)
+        w_codes = tiles("w_codes", [[P, n * QT] for n in slots], U32)
+        w_scales = tiles("w_scales", [[P, n * QT] for n in slots], U8)
+        den = tiles("den", [[P, n, 1] for n in slots], F32)
+        rden = tiles("rden", [[P, n] for n in slots], F32)
+        res = tiles("res", [[P, n, E] for n in slots], F32)
 
-        def load_k(i):
-            g, c = divmod(i, 2)
-            nc.sync.dma_start(out=k_raw[i][:], in_=k_rows[g * P : (g + 1) * P, :, c * 256 : (c + 1) * 256])
+        def place(grp, z):
+            g, lo, hi = GROUPS[grp]
+            return g, z % 2, lo + z // 2
+
+        def load_k(g):
+            nc.sync.dma_start(out=k_raw[g][:], in_=k_rows[g * P : (g + 1) * P])
 
         def load_q(i):
-            g, a, b = q_loads[i]
-            nc.sync.dma_start(out=q_raw[i][:], in_=q_rows[g * P : (g + 1) * P, :, a * QT : b * QT])
+            g, lo, hi = Q_LOADS[i]
+            nc.sync.dma_start(out=q_raw[i][:], in_=q_rows[g * P : (g + 1) * P, :, lo * QT : hi * QT])
 
         def load_v(g):
             nc.sync.dma_start(
@@ -100,38 +102,65 @@ def tile_rows_a_relu2_cap_gate_kernel(tc, qT, kT, t, v, og, out):
             )
 
         def load_og(i):
-            h, a, b = og_loads[i]
-            nc.sync.dma_start(out=og_raw[i][:], in_=og[h, a * QT : b * QT, :].rearrange("(m p) e -> p m e", p=P))
+            h0, h1, m0, m1 = OG_LOADS[i]
+            if h1 - h0 == 1:
+                src = og[h0, m0 * QT : m1 * QT, :].rearrange("(m p) e -> p m e", p=P)
+            else:
+                src = og[h0:h1, m0 * QT : m1 * QT, :].rearrange("h p e -> p h e")
+            nc.sync.dma_start(out=og_raw[i][:], in_=src)
+
+        def load_t():
+            nc.sync.dma_start(out=t_sb[:], in_=t.rearrange("(p j) o -> p (j o)", j=PACK))
+
+        def make_half():
+            nc.gpsimd.memset(zero[:], 0.0)
+            nc.scalar.activation(out=half[:], in_=zero[:], func=ACT.Sigmoid)
+
+        def root():
+            nc.scalar.activation(out=t_abs[:], in_=t_sb[:], func=ACT.Abs, scale=CAP * CAP)
+            nc.gpsimd.tensor_tensor(out=t_root[:], in0=t_abs[:], in1=half[:], op=ALU.pow)
+
+        def sign(step):
+            if step == 0:
+                nc.vector.tensor_scalar(out=t_pos[:], in0=t_sb[:], scalar1=0.0, scalar2=2.0, op0=ALU.is_ge, op1=ALU.mult)
+            else:
+                nc.vector.tensor_scalar(out=t_sign[:], in0=t_pos[:], scalar1=-1.0, scalar2=None, op0=ALU.add)
 
         def sigmoid(i):
             nc.scalar.activation(out=gate[i][:], in_=og_raw[i][:], func=ACT.Sigmoid)
 
         def gate_of(h, m):
-            i = [n for n, (hh, a, b) in enumerate(og_loads) if hh == h and a <= m < b][0]
-            return gate[i][:, m - og_loads[i][1], :]
+            i = [n for n, (h0, h1, m0, m1) in enumerate(OG_LOADS) if h0 <= h < h1 and m0 <= m < m1][0]
+            h0, h1, m0, m1 = OG_LOADS[i]
+            return gate[i][:, (h - h0) * (m1 - m0) + m - m0, :]
 
         def quantize(codes, scales, src):
-            nc.vector.quantize_mx(out=codes[:].bitcast(FP8X4), scales=scales[:], in_=src)
+            nc.vector.quantize_mx(out=codes.bitcast(FP8X4), scales=scales, in_=src)
 
-        def copy_k(i):
-            g, c = divmod(i, 2)
-            nc.vector.tensor_copy(
-                out=k_bf[g][:, :, c * 64 : (c + 1) * 64, :].rearrange("p r s j -> p s j r"),
-                in_=k_raw[i][:].rearrange("p j (s r) -> p s j r", r=PACK),
+        def copy_k(g, part):
+            lo, hi, copy = [
+                (0, K_SPLIT, nc.vector.tensor_copy),
+                (K_SPLIT, P, nc.scalar.copy),
+                (0, P // 2, nc.vector.tensor_copy),
+                (P // 2, P, nc.vector.tensor_copy),
+            ][part]
+            copy(
+                out=k_bf[g][:, :, lo:hi, :].rearrange("p r s j -> p s j r"),
+                in_=k_raw[g][:, :, lo * PACK : hi * PACK].rearrange("p j (s r) -> p s j r", r=PACK),
             )
 
         def quant_k(g):
-            quantize(k_codes[g], k_scales[g], k_bf[g][:].rearrange("p r s j -> p (r s j)"))
+            quantize(k_codes[g][:], k_scales[g][:], k_bf[g][:].rearrange("p r s j -> p (r s j)"))
 
-        def copy_q(i):
-            copy = nc.scalar.copy if i in Q_COPY_ON_SCALAR else nc.vector.tensor_copy
+        def copy_q(i, on_scalar):
+            copy = nc.scalar.copy if on_scalar else nc.vector.tensor_copy
             copy(
                 out=q_bf[i][:].rearrange("p (c i) j -> p c j i", i=2),
                 in_=q_raw[i][:].rearrange("p j (c i) -> p c j i", i=2),
             )
 
         def quant_q(i):
-            quantize(q_codes[i], q_scales[i], q_bf[i][:].rearrange("p c j -> p (c j)"))
+            quantize(q_codes[i][:], q_scales[i][:], q_bf[i][:].rearrange("p c j -> p (c j)"))
 
         def copy_v(h):
             g, a = divmod(h, 2)
@@ -143,17 +172,17 @@ def tile_rows_a_relu2_cap_gate_kernel(tc, qT, kT, t, v, og, out):
             )
 
         def quant_v(g):
-            quantize(v_codes[g], v_scales[g], v_bf[g][:].rearrange("p h e j -> p (h e j)"))
+            quantize(v_codes[g][:], v_scales[g][:], v_bf[g][:].rearrange("p h e j -> p (h e j)"))
 
-        def scores(u, a):
-            g, m = divmod(u, TILES)
-            i = [n for n, (gg, lo, hi) in enumerate(q_loads) if gg == g and lo <= m < hi][0]
-            q_cols = slice((m - q_loads[i][1]) * QT, (m - q_loads[i][1] + 1) * QT)
+        def scores(grp, z):
+            g, a, m = place(grp, z)
+            i = [n for n, (gg, lo, hi) in enumerate(Q_LOADS) if gg == g and lo <= m < hi][0]
+            q_cols = slice((m - Q_LOADS[i][1]) * QT, (m - Q_LOADS[i][1] + 1) * QT)
             rows = slice(a * ROWS, (a + 1) * ROWS)
             for r in range(PACK):
                 cols = slice(r * P, (r + 1) * P)
                 nc.tensor.matmul_mx(
-                    out=score[a][u % SCORE_BANKS][:, r, :],
+                    out=score[a][m % SCORE_BANKS][:, r, :],
                     lhsT=k_codes[g][rows, cols].bitcast(FP8X4),
                     lhsT_scale=k_scales[g][rows, cols],
                     rhs=q_codes[i][rows, q_cols].bitcast(FP8X4),
@@ -162,95 +191,80 @@ def tile_rows_a_relu2_cap_gate_kernel(tc, qT, kT, t, v, og, out):
                     stop=True,
                 )
 
-        def cap(u, a):
+        def cap(grp, z):
+            g, a, m = place(grp, z)
             nc.scalar.activation(
-                out=th[u][:, :, a * QT : (a + 1) * QT],
-                in_=score[a][u % SCORE_BANKS][:],
+                out=th[grp][:, :, z * QT : (z + 1) * QT],
+                in_=score[a][m % SCORE_BANKS][:],
                 func=ACT.Tanh,
                 scale=1.0 / CAP,
             )
 
-        def relu_scale(u, r):
+        def relu_scale(grp, r):
             nc.vector.tensor_scalar(
-                out=root_w[u][:, r, :],
-                in0=th[u][:, r, :],
+                out=root_w[grp][:, r, :],
+                in0=th[grp][:, r, :],
                 scalar1=0.0,
                 scalar2=t_root[:, r : r + 1],
                 op0=ALU.max,
                 op1=ALU.mult,
             )
 
-        def square(u):
-            src = root_w[u][:].rearrange("p r (c i) -> p c r i", i=2)
-            dst = w_bf[u][:].rearrange("p (c i) r -> p c r i", i=2)
-            if u in SQUARE_ON_VECTOR:
-                nc.vector.tensor_tensor(out=dst, in0=src, in1=src, op=ALU.mult)
-            else:
+        def square(grp, lo, hi, on_scalar):
+            src = root_w[grp][:, :, lo * QT : hi * QT].rearrange("p r (c i) -> p c r i", i=2)
+            dst = w_bf[grp][:, lo * QT : hi * QT, :].rearrange("p (c i) r -> p c r i", i=2)
+            if on_scalar:
                 nc.scalar.activation(out=dst, in_=src, func=ACT.Square)
+            else:
+                nc.vector.tensor_tensor(out=dst, in0=src, in1=src, op=ALU.mult)
 
-        def quant_w(u):
-            quantize(w_codes[u], w_scales[u], w_bf[u][:].rearrange("p c r -> p (c r)"))
+        def quant_w(grp, lo, hi):
+            cols = slice(lo * QT, hi * QT)
+            quantize(w_codes[grp][:, cols], w_scales[grp][:, cols], w_bf[grp][:, cols, :].rearrange("p c r -> p (c r)"))
 
-        def y_of(u):
-            b, s = u % Y_BANKS, 2 * ((u // Y_BANKS) % 2)
-            return y_ps[b][:, s : s + 2, :]
-
-        def values(u):
-            g = u // TILES
-            for a in range(2):
-                cols = slice(a * P, (a + 1) * P)
+        def values(grp, lo, hi):
+            for z in range(lo, hi):
+                g, a, m = place(grp, z)
+                cols = slice(z * QT, (z + 1) * QT)
+                v_cols = slice(a * E, (a + 1) * E)
                 nc.tensor.matmul_mx(
-                    out=y_of(u)[:, a, :],
-                    lhsT=w_codes[u][:, cols].bitcast(FP8X4),
-                    lhsT_scale=w_scales[u][:, cols],
-                    rhs=v_codes[g][:, cols].bitcast(FP8X4),
-                    rhs_scale=v_scales[g][:, cols],
+                    out=y_ps[grp % Y_BANKS][:, z, :],
+                    lhsT=w_codes[grp][:, cols].bitcast(FP8X4),
+                    lhsT_scale=w_scales[grp][:, cols],
+                    rhs=v_codes[g][:, v_cols].bitcast(FP8X4),
+                    rhs_scale=v_scales[g][:, v_cols],
                     start=True,
                     stop=True,
                 )
 
-        def den_add(u):
+        def den_add(grp):
             nc.vector.tensor_scalar(
-                out=den[u][:], in0=y_of(u)[:, :, E - 1 : E], scalar1=1.0, scalar2=None, op0=ALU.add
+                out=den[grp][:], in0=y_ps[grp % Y_BANKS][:, : slots[grp], E - 1 : E], scalar1=1.0, scalar2=None, op0=ALU.add
             )
 
-        def den_recip(u):
-            nc.vector.reciprocal(out=rden[u][:], in_=den[u][:].rearrange("p a o -> p (a o)"))
+        def den_recip(grp):
+            nc.vector.reciprocal(out=rden[grp][:], in_=den[grp][:].rearrange("p a o -> p (a o)"))
 
-        def finish(u, a):
-            g, m = divmod(u, TILES)
+        def finish(grp, z):
+            g, a, m = place(grp, z)
             nc.vector.scalar_tensor_tensor(
-                out=res[u][:, a, :],
-                in0=y_of(u)[:, a, :],
-                scalar=rden[u][:, a : a + 1],
+                out=res[grp][:, z, :],
+                in0=y_ps[grp % Y_BANKS][:, z, :],
+                scalar=rden[grp][:, z : z + 1],
                 in1=gate_of(2 * g + a, m),
                 op0=ALU.mult,
                 op1=ALU.mult,
             )
 
-        def store(u):
-            g, m = divmod(u, TILES)
+        def store(grp, lo, hi):
+            g, a, m = place(grp, lo)
             nc.sync.dma_start(
-                out=out[2 * g : 2 * g + 2, m * QT : (m + 1) * QT, :].rearrange("h p e -> p h e"),
-                in_=res[u][:],
+                out=out[2 * g + a : 2 * g + a + hi - lo, m * QT : (m + 1) * QT, :].rearrange("h p e -> p h e"),
+                in_=res[grp][:, lo:hi, :],
             )
 
-        def load_t():
-            nc.sync.dma_start(out=t_sb[:], in_=t.rearrange("(p j) o -> p (j o)", j=PACK))
-
-        def root():
-            nc.gpsimd.memset(half[:], 0.5)
-            nc.scalar.activation(out=t_abs[:], in_=t_sb[:], func=ACT.Abs, scale=CAP * CAP)
-            nc.gpsimd.tensor_tensor(out=t_root[:], in0=t_abs[:], in1=half[:], op=ALU.pow)
-
-        def sign(step):
-            if step == 0:
-                nc.vector.tensor_scalar(out=t_pos[:], in0=t_sb[:], scalar1=0.0, scalar2=2.0, op0=ALU.is_ge, op1=ALU.mult)
-            else:
-                nc.vector.tensor_scalar(out=t_sign[:], in0=t_pos[:], scalar1=-1.0, scalar2=None, op0=ALU.add)
-
         steps = {
-            "lk": load_k, "lq": load_q, "lv": load_v, "lo": load_og, "lt": load_t, "root": root, "sign": sign,
+            "lk": load_k, "lq": load_q, "lv": load_v, "lo": load_og, "lt": load_t, "half": make_half, "root": root, "sign": sign,
             "sig": sigmoid, "ck": copy_k, "qk": quant_k, "cq": copy_q, "qq": quant_q, "cv": copy_v, "qv": quant_v,
             "sc": scores, "cap": cap, "rs": relu_scale, "sq": square, "qw": quant_w, "val": values,
             "da": den_add, "dr": den_recip, "fin": finish, "st": store,

@@ -25,7 +25,7 @@ GROUPS = [(0, 0, 1), (0, 1, 2), (0, 2, 4), (1, 0, 2), (1, 2, 3), (1, 3, 4)]
 Q_LOADS = [(0, 0, 1), (0, 1, 2), (0, 2, 4), (1, 0, 2), (1, 2, 4)]
 OG_LOADS = [(0, 2, 0, 1), (0, 2, 1, 2), (0, 1, 2, 4), (1, 2, 2, 4), (2, 3, 0, 2), (3, 4, 0, 2), (2, 4, 2, 3), (2, 4, 3, 4)]
 K_SPLIT = 88
-ORDER = "lk:0 lq:0 lt: lq:1 lq:2 lk:1 lq:3 lq:4 lv:0 lo:0 lo:1 lv:1 lo:2 lo:3 lo:4 lo:5 lo:6 lo:7 half: ck:00 ck:01 cq:01 root: qk:0 qq:0 sc:00 sc:01 cq:11 sign:0 qq:1 sc:10 sc:11 cap:00 cap:01 cq:20 sign:1 cap:10 cap:11 rs:00 rs:01 qq:2 rs:02 rs:03 sc:20 sc:21 sc:22 sc:23 sq:0021 rs:10 rs:11 rs:12 rs:13 ck:12 ck:13 cq:30 qk:1 qq:3 cap:20 cap:21 cap:22 cap:23 sq:1021 sc:30 sc:31 sc:32 sc:33 cq:40 rs:20 rs:21 qq:4 cv:0 rs:22 rs:23 cv:1 qw:002 qv:0 qw:102 cap:30 cap:31 cap:32 cap:33 sc:40 sc:41 val:002 val:102 sc:50 sc:51 sq:2021 sq:2241 sig:0 cv:2 da:0 da:1 rs:30 dr:0 dr:1 rs:31 rs:32 rs:33 qw:204 val:204 cap:40 cap:41 cap:50 cap:51 sig:1 cv:3 rs:40 rs:41 rs:42 rs:43 da:2 fin:00 fin:01 st:002 dr:2 sq:4020 sq:3021 sq:3241 sig:2 sig:3 rs:50 rs:51 rs:52 rs:53 qv:1 qw:402 val:402 fin:10 fin:11 st:102 qw:304 val:304 sq:5021 sig:4 sig:5 sig:6 sig:7 da:4 fin:20 fin:21 st:202 da:3 dr:4 fin:22 fin:23 st:224 dr:3 qw:502 val:502 fin:30 fin:31 st:302 fin:32 da:5 fin:33 st:324 dr:5 fin:40 fin:41 st:402 fin:50 fin:51 st:502".split(" ")
+ORDER = "lk:0 lq:0 lq:1 lt: lq:2 lk:1 lq:3 lq:4 lv:0 lo:0 lo:1 lv:1 lo:2 lo:3 lo:4 lo:5 lo:6 lo:7 half: ck:00 ck:01 cq:01 qk:0 qq:0 sc:00 cq:11 root: sign:0 qq:1 sc:10 cap:00 cap:01 cq:20 sign:1 cap:10 cap:11 rs:00 rs:01 qq:2 rs:02 rs:03 sc:20 sc:21 sq:0021 rs:10 rs:11 rs:12 rs:13 ck:12 ck:13 cq:30 qk:1 qq:3 cap:20 cap:21 cap:22 cap:23 sq:1021 sc:30 sc:31 cq:40 rs:20 rs:21 qq:4 cv:0 rs:22 rs:23 cv:1 qw:002 qv:0 qw:102 cap:30 cap:31 cap:32 cap:33 sc:40 val:002 val:102 sc:50 sq:2021 sq:2241 sig:0 cv:2 da:0 da:1 rs:30 dr:0 dr:1 rs:31 rs:32 rs:33 qw:204 val:204 cap:40 cap:41 cap:50 cap:51 sig:1 cv:3 rs:40 rs:41 rs:42 rs:43 da:2 fin:00 fin:01 st:002 dr:2 sq:4020 sq:3021 sq:3241 sig:2 sig:3 rs:50 rs:51 rs:52 rs:53 qv:1 qw:402 val:402 fin:10 fin:11 st:102 qw:304 val:304 sq:5021 sig:4 sig:5 sig:6 sig:7 da:4 fin:20 fin:21 st:202 da:3 dr:4 fin:22 fin:23 st:224 dr:3 qw:502 val:502 fin:30 fin:31 st:302 fin:32 da:5 fin:33 st:324 dr:5 fin:40 fin:41 st:402 fin:50 st:501 fin:51 st:512".split(" ")
 
 
 def tile_rows_a_relu2_cap_gate_kernel(tc, qT, kT, t, v, og, out):
@@ -175,21 +175,22 @@ def tile_rows_a_relu2_cap_gate_kernel(tc, qT, kT, t, v, og, out):
             quantize(v_codes[g][:], v_scales[g][:], v_bf[g][:].rearrange("p h e j -> p (h e j)"))
 
         def scores(grp, z):
-            g, a, m = place(grp, z)
+            g, a, m = place(grp, 2 * z)
             i = [n for n, (gg, lo, hi) in enumerate(Q_LOADS) if gg == g and lo <= m < hi][0]
             q_cols = slice((m - Q_LOADS[i][1]) * QT, (m - Q_LOADS[i][1] + 1) * QT)
-            rows = slice(a * ROWS, (a + 1) * ROWS)
             for r in range(PACK):
                 cols = slice(r * P, (r + 1) * P)
-                nc.tensor.matmul_mx(
-                    out=score[a][m % SCORE_BANKS][:, r, :],
-                    lhsT=k_codes[g][rows, cols].bitcast(FP8X4),
-                    lhsT_scale=k_scales[g][rows, cols],
-                    rhs=q_codes[i][rows, q_cols].bitcast(FP8X4),
-                    rhs_scale=q_scales[i][rows, q_cols],
-                    start=True,
-                    stop=True,
-                )
+                for a in range(2):
+                    rows = slice(a * ROWS, (a + 1) * ROWS)
+                    nc.tensor.matmul_mx(
+                        out=score[a][m % SCORE_BANKS][:, r, :],
+                        lhsT=k_codes[g][rows, cols].bitcast(FP8X4),
+                        lhsT_scale=k_scales[g][rows, cols],
+                        rhs=q_codes[i][rows, q_cols].bitcast(FP8X4),
+                        rhs_scale=q_scales[i][rows, q_cols],
+                        start=True,
+                        stop=True,
+                    )
 
         def cap(grp, z):
             g, a, m = place(grp, z)

@@ -25,7 +25,7 @@ GROUPS = [(0, 0, 1), (0, 1, 2), (0, 2, 4), (1, 0, 2), (1, 2, 3), (1, 3, 4)]
 Q_LOADS = [(0, 0, 1), (0, 1, 2), (0, 2, 4), (1, 0, 2), (1, 2, 4)]
 OG_LOADS = [(0, 2, 0, 1), (0, 2, 1, 2), (0, 1, 2, 4), (1, 2, 2, 4), (2, 3, 0, 2), (3, 4, 0, 2), (2, 4, 2, 3), (2, 4, 3, 4)]
 K_SPLIT = 88
-ORDER = "lk:0 lq:0 lq:1 lt: lq:2 lk:1 lq:3 lq:4 lv:0 lo:0 lo:1 lv:1 lo:2 lo:3 lo:4 lo:5 lo:6 lo:7 half: ck:00 ck:01 cq:01 qk:0 qq:0 sc:00 cq:11 root: sign:0 qq:1 sc:10 cap:00 cap:01 cq:20 sign:1 cap:10 cap:11 rs:00 rs:01 qq:2 rs:02 rs:03 sc:20 sc:21 sq:0021 rs:10 rs:11 rs:12 rs:13 ck:12 ck:13 cq:30 qk:1 qq:3 cap:20 cap:21 cap:22 cap:23 sq:1021 sc:30 sc:31 cq:40 rs:20 rs:21 qq:4 cv:0 rs:22 rs:23 cv:1 qw:002 qv:0 qw:102 cap:30 cap:31 cap:32 cap:33 sc:40 val:002 val:102 sc:50 sq:2021 sq:2241 sig:0 cv:2 da:0 da:1 rs:30 dr:0 dr:1 rs:31 rs:32 rs:33 qw:204 val:204 cap:40 cap:41 cap:50 cap:51 sig:1 cv:3 rs:40 rs:41 rs:42 rs:43 da:2 fin:00 fin:01 st:002 dr:2 sq:4020 sq:3021 sq:3241 sig:2 sig:3 rs:50 rs:51 rs:52 rs:53 qv:1 qw:402 val:402 fin:10 fin:11 st:102 qw:304 val:304 sq:5021 sig:4 sig:5 sig:6 sig:7 da:4 fin:20 fin:21 st:202 da:3 dr:4 fin:22 fin:23 st:224 dr:3 qw:502 val:502 fin:30 fin:31 st:302 fin:32 da:5 fin:33 st:324 dr:5 fin:40 fin:41 st:402 fin:50 st:501 fin:51 st:512".split(" ")
+ORDER = "lt: lk:0 lq:0 lq:1 lq:2 lk:1 lq:3 lq:4 lv:0 lo:0 lo:1 lv:1 lo:2 lo:3 lo:4 lo:5 lo:6 lo:7 half: root: sign:0 sign:1 ck:00 ck:01 cq:01 qk:0 qq:0 sc:00 cq:11 qq:1 sc:10 cap:00 cap:01 cq:20 cap:10 cap:11 rs:00 qq:2 rs:01 rs:02 rs:03 sc:20 sc:21 sq:0021 rs:10 rs:11 rs:12 rs:13 ck:12 ck:13 cq:30 qk:1 qq:3 cap:20 cap:21 cap:22 cap:23 sq:1021 sc:30 sc:31 cq:40 rs:20 rs:21 qq:4 cv:0 rs:22 rs:23 cv:1 qw:002 qv:0 qw:102 cap:30 cap:31 cap:32 cap:33 sc:40 val:002 val:102 sc:50 sq:2021 sq:2241 sig:0 cv:2 da:0 da:1 rs:30 dr:0 dr:1 rs:31 rs:32 rs:33 qw:204 val:204 cap:40 cap:41 cap:50 cap:51 sig:1 cv:3 rs:40 rs:41 rs:42 rs:43 da:2 fin:00 fin:01 st:002 dr:2 sq:4020 sq:3021 sq:3241 sig:2 sig:3 rs:50 rs:51 rs:52 rs:53 qv:1 fin:10 fin:11 st:102 qw:304 val:304 qw:402 val:402 sq:5021 sig:4 sig:5 sig:6 sig:7 fin:20 fin:21 st:202 da:3 fin:22 da:4 fin:23 st:224 dr:3 dr:4 qw:502 val:502 fin:30 fin:31 st:302 fin:32 da:5 fin:33 st:324 dr:5 fin:40 fin:41 st:402 fin:50 st:501 fin:51 st:512".split(" ")
 
 
 def tile_rows_a_relu2_cap_gate_kernel(tc, qT, kT, t, v, og, out):

@@ -16,16 +16,21 @@ ACT = mybir.ActivationFunctionType
 
 P = 128
 PACK = 4
-ROWS = 64
+SIDES = 2
+PAIRS = H // SIDES
+ROWS = P // SIDES
 QT = 128
-TILES = NQ // QT
+RUN = 2
 SCORE_BANKS = 2
 Y_BANKS = 4
+
 GROUPS = [(0, 0, 1), (0, 1, 2), (0, 2, 4), (1, 0, 2), (1, 2, 3), (1, 3, 4)]
 Q_LOADS = [(0, 0, 1), (0, 1, 2), (0, 2, 4), (1, 0, 2), (1, 2, 4)]
-OG_LOADS = [(0, 2, 0, 1), (0, 2, 1, 2), (0, 1, 2, 4), (1, 2, 2, 4), (2, 3, 0, 2), (3, 4, 0, 2), (2, 4, 2, 3), (2, 4, 3, 4)]
+OG_LOADS = [
+    (0, 2, 0, 1), (0, 2, 1, 2), (0, 1, 2, 4), (1, 2, 2, 4),
+    (2, 4, 2, 3), (2, 3, 0, 2), (3, 4, 0, 2), (2, 4, 3, 4),
+]
 K_SPLIT = 88
-ORDER = "lt: lk:0 lq:0 lq:1 lq:2 lk:1 lq:3 lq:4 lv:0 lo:0 lo:1 lv:1 lo:2 lo:3 lo:4 lo:5 lo:6 lo:7 half: root: sign:0 sign:1 ck:00 ck:01 cq:01 qk:0 qq:0 sc:00 cq:11 qq:1 sc:10 cap:00 cap:01 cq:20 cap:10 cap:11 rs:00 qq:2 rs:01 rs:02 rs:03 sc:20 sc:21 sq:0021 rs:10 rs:11 rs:12 rs:13 ck:12 ck:13 cq:30 qk:1 qq:3 cap:20 cap:21 cap:22 cap:23 sq:1021 sc:30 sc:31 cq:40 rs:20 rs:21 qq:4 cv:0 rs:22 rs:23 cv:1 qw:002 qv:0 qw:102 cap:30 cap:31 cap:32 cap:33 sc:40 val:002 val:102 sc:50 sq:2021 sq:2241 sig:0 cv:2 da:0 da:1 rs:30 dr:0 dr:1 rs:31 rs:32 rs:33 qw:204 val:204 cap:40 cap:41 cap:50 cap:51 sig:1 cv:3 rs:40 rs:41 rs:42 rs:43 da:2 fin:00 fin:01 st:002 dr:2 sq:4020 sq:3021 sq:3241 sig:2 sig:3 rs:50 rs:51 rs:52 rs:53 qv:1 fin:10 fin:11 st:102 qw:304 val:304 qw:402 val:402 sq:5021 sig:4 sig:5 sig:6 sig:7 fin:20 fin:21 st:202 da:3 fin:22 da:4 fin:23 st:224 dr:3 dr:4 qw:502 val:502 fin:30 fin:31 st:302 fin:32 da:5 fin:33 st:324 dr:5 fin:40 fin:41 st:402 fin:50 st:501 fin:51 st:512".split(" ")
 
 
 def tile_rows_a_relu2_cap_gate_kernel(tc, qT, kT, t, v, og, out):
@@ -38,200 +43,181 @@ def tile_rows_a_relu2_cap_gate_kernel(tc, qT, kT, t, v, og, out):
         ps = ctx.enter_context(tc.psum_pool(name="ps", bufs=1))
 
         def tiles(name, shapes, dtype):
-            return [sb.tile(shape, dtype, name=name + str(i), align_bytes=64) for i, shape in enumerate(shapes)]
+            return [sb.tile(shape, dtype, name=name + str(n), align_bytes=64) for n, shape in enumerate(shapes)]
 
         score = [
             [ps.tile([P, PACK, QT], F32, name="score%d_%d" % (a, b)) for b in range(SCORE_BANKS)]
-            for a in range(2)
+            for a in range(SIDES)
         ]
-        y_ps = [ps.tile([P, PACK, E], F32, name="y%d" % b) for b in range(Y_BANKS)]
+        y_ps = [ps.tile([P, 2 * SIDES, E], F32, name="y%d" % b) for b in range(Y_BANKS)]
 
         t_sb = sb.tile([P, PACK], F32, name="t_sb")
-        t_pos = sb.tile([P, PACK], F32, name="t_pos")
+        t_step = sb.tile([P, PACK], F32, name="t_step")
         t_sign = sb.tile([P, PACK], F32, name="t_sign")
         t_abs = sb.tile([P, PACK], F32, name="t_abs")
         zero = sb.tile([P, PACK], F32, name="zero")
         half = sb.tile([P, PACK], F32, name="half")
         t_root = sb.tile([P, PACK], F32, name="t_root")
 
-        k_raw = tiles("k_raw", [[P, PACK, N]] * 2, F32)
-        k_bf = tiles("k_bf", [[P, PACK, P, PACK]] * 2, BF16)
-        k_codes = tiles("k_codes", [[P, N]] * 2, U32)
-        k_scales = tiles("k_scales", [[P, N]] * 2, U8)
+        k_raw = tiles("k_raw", [[P, PACK, N]] * PAIRS, F32)
+        k_bf = tiles("k_bf", [[P, PACK, P, PACK]] * PAIRS, BF16)
+        k_codes = tiles("k_codes", [[P, N]] * PAIRS, U32)
+        k_scales = tiles("k_scales", [[P, N]] * PAIRS, U8)
 
-        q_width = [(hi - lo) * QT for g, lo, hi in Q_LOADS]
-        q_raw = tiles("q_raw", [[P, PACK, n] for n in q_width], F32)
-        q_bf = tiles("q_bf", [[P, n, PACK] for n in q_width], BF16)
-        q_codes = tiles("q_codes", [[P, n] for n in q_width], U32)
-        q_scales = tiles("q_scales", [[P, n] for n in q_width], U8)
+        q_width = [(end - first) * QT for g, first, end in Q_LOADS]
+        q_raw = tiles("q_raw", [[P, PACK, width] for width in q_width], F32)
+        q_bf = tiles("q_bf", [[P, width, PACK] for width in q_width], BF16)
+        q_codes = tiles("q_codes", [[P, width] for width in q_width], U32)
+        q_scales = tiles("q_scales", [[P, width] for width in q_width], U8)
 
-        v_raw = tiles("v_raw", [[P, 2, PACK, E]] * 2, F32)
-        v_bf = tiles("v_bf", [[P, 2, E, PACK]] * 2, BF16)
-        v_codes = tiles("v_codes", [[P, 2 * E]] * 2, U32)
-        v_scales = tiles("v_scales", [[P, 2 * E]] * 2, U8)
+        v_raw = tiles("v_raw", [[P, SIDES, PACK, E]] * PAIRS, F32)
+        v_bf = tiles("v_bf", [[P, SIDES, E, PACK]] * PAIRS, BF16)
+        v_codes = tiles("v_codes", [[P, SIDES * E]] * PAIRS, U32)
+        v_scales = tiles("v_scales", [[P, SIDES * E]] * PAIRS, U8)
 
-        og_shape = [[P, (h1 - h0) * (m1 - m0), E] for h0, h1, m0, m1 in OG_LOADS]
-        og_raw = tiles("og_raw", og_shape, F32)
-        gate = tiles("gate", og_shape, F32)
+        og_shapes = [[P, (h_end - h) * (end - first), E] for h, h_end, first, end in OG_LOADS]
+        og_raw = tiles("og_raw", og_shapes, F32)
+        gate = tiles("gate", og_shapes, F32)
 
-        slots = [2 * (hi - lo) for g, lo, hi in GROUPS]
-        th = tiles("th", [[P, PACK, n * QT] for n in slots], F32)
-        root_w = tiles("root_w", [[P, PACK, n * QT] for n in slots], F32)
-        w_bf = tiles("w_bf", [[P, n * QT, PACK] for n in slots], BF16)
-        w_codes = tiles("w_codes", [[P, n * QT] for n in slots], U32)
-        w_scales = tiles("w_scales", [[P, n * QT] for n in slots], U8)
-        den = tiles("den", [[P, n, 1] for n in slots], F32)
-        rden = tiles("rden", [[P, n] for n in slots], F32)
-        res = tiles("res", [[P, n, E] for n in slots], F32)
+        items = [SIDES * (end - first) for g, first, end in GROUPS]
+        capped = tiles("capped", [[P, PACK, count * QT] for count in items], F32)
+        root_w = tiles("root_w", [[P, PACK, count * QT] for count in items], F32)
+        w_bf = tiles("w_bf", [[P, count * QT, PACK] for count in items], BF16)
+        w_codes = tiles("w_codes", [[P, count * QT] for count in items], U32)
+        w_scales = tiles("w_scales", [[P, count * QT] for count in items], U8)
+        den = tiles("den", [[P, count, 1] for count in items], F32)
+        rden = tiles("rden", [[P, count] for count in items], F32)
+        res = tiles("res", [[P, count, E] for count in items], F32)
 
         def place(grp, z):
-            g, lo, hi = GROUPS[grp]
-            return g, z % 2, lo + z // 2
+            g, first, end = GROUPS[grp]
+            return g, z % SIDES, first + z // SIDES
 
         def load_k(g):
             nc.sync.dma_start(out=k_raw[g][:], in_=k_rows[g * P : (g + 1) * P])
 
-        def load_q(i):
-            g, lo, hi = Q_LOADS[i]
-            nc.sync.dma_start(out=q_raw[i][:], in_=q_rows[g * P : (g + 1) * P, :, lo * QT : hi * QT])
+        def load_q(n):
+            g, first, end = Q_LOADS[n]
+            nc.sync.dma_start(out=q_raw[n][:], in_=q_rows[g * P : (g + 1) * P, :, first * QT : end * QT])
 
         def load_v(g):
             nc.sync.dma_start(
-                out=v_raw[g][:].rearrange("p h j e -> p h (j e)"),
-                in_=v[2 * g : 2 * g + 2].rearrange("h (p j) e -> p h (j e)", j=PACK),
+                out=v_raw[g][:].rearrange("s a r e -> s a (r e)"),
+                in_=v[SIDES * g : SIDES * (g + 1)].rearrange("a (s r) e -> s a (r e)", r=PACK),
             )
 
-        def load_og(i):
-            h0, h1, m0, m1 = OG_LOADS[i]
-            if h1 - h0 == 1:
-                src = og[h0, m0 * QT : m1 * QT, :].rearrange("(m p) e -> p m e", p=P)
+        def load_og(n):
+            h, h_end, first, end = OG_LOADS[n]
+            if h_end - h == 1:
+                src = og[h, first * QT : end * QT, :].rearrange("(m p) e -> p m e", p=P)
             else:
-                src = og[h0:h1, m0 * QT : m1 * QT, :].rearrange("h p e -> p h e")
-            nc.sync.dma_start(out=og_raw[i][:], in_=src)
-
-        def load_t():
-            nc.sync.dma_start(out=t_sb[:], in_=t.rearrange("(p j) o -> p (j o)", j=PACK))
-
-        def make_half():
-            nc.gpsimd.memset(zero[:], 0.0)
-            nc.scalar.activation(out=half[:], in_=zero[:], func=ACT.Sigmoid)
-
-        def root():
-            nc.scalar.activation(out=t_abs[:], in_=t_sb[:], func=ACT.Abs, scale=CAP * CAP)
-            nc.gpsimd.tensor_tensor(out=t_root[:], in0=t_abs[:], in1=half[:], op=ALU.pow)
-
-        def sign(step):
-            if step == 0:
-                nc.vector.tensor_scalar(out=t_pos[:], in0=t_sb[:], scalar1=0.0, scalar2=2.0, op0=ALU.is_ge, op1=ALU.mult)
-            else:
-                nc.vector.tensor_scalar(out=t_sign[:], in0=t_pos[:], scalar1=-1.0, scalar2=None, op0=ALU.add)
-
-        def sigmoid(i):
-            nc.scalar.activation(out=gate[i][:], in_=og_raw[i][:], func=ACT.Sigmoid)
-
-        def gate_of(h, m):
-            i = [n for n, (h0, h1, m0, m1) in enumerate(OG_LOADS) if h0 <= h < h1 and m0 <= m < m1][0]
-            h0, h1, m0, m1 = OG_LOADS[i]
-            return gate[i][:, (h - h0) * (m1 - m0) + m - m0, :]
+                src = og[h:h_end, first * QT : end * QT, :].rearrange("h p e -> p h e")
+            nc.sync.dma_start(out=og_raw[n][:], in_=src)
 
         def quantize(codes, scales, src):
             nc.vector.quantize_mx(out=codes.bitcast(FP8X4), scales=scales, in_=src)
 
-        def copy_k(g, part):
-            lo, hi, copy = [
-                (0, K_SPLIT, nc.vector.tensor_copy),
-                (K_SPLIT, P, nc.scalar.copy),
-                (0, P // 2, nc.vector.tensor_copy),
-                (P // 2, P, nc.vector.tensor_copy),
-            ][part]
+        def copy_k(g, s_first, s_end, copy):
             copy(
-                out=k_bf[g][:, :, lo:hi, :].rearrange("p r s j -> p s j r"),
-                in_=k_raw[g][:, :, lo * PACK : hi * PACK].rearrange("p j (s r) -> p s j r", r=PACK),
+                out=k_bf[g][:, :, s_first:s_end, :].rearrange("p r s j -> p s j r"),
+                in_=k_raw[g][:, :, s_first * PACK : s_end * PACK].rearrange("p j (s r) -> p s j r", r=PACK),
             )
 
-        def quant_k(g):
-            quantize(k_codes[g][:], k_scales[g][:], k_bf[g][:].rearrange("p r s j -> p (r s j)"))
-
-        def copy_q(i, on_scalar):
-            copy = nc.scalar.copy if on_scalar else nc.vector.tensor_copy
-            copy(
-                out=q_bf[i][:].rearrange("p (c i) j -> p c j i", i=2),
-                in_=q_raw[i][:].rearrange("p j (c i) -> p c j i", i=2),
+        def quant_k(g, r_first, r_end):
+            cols = slice(r_first * P, r_end * P)
+            quantize(
+                k_codes[g][:, cols],
+                k_scales[g][:, cols],
+                k_bf[g][:, r_first:r_end].rearrange("p r s j -> p (r s j)"),
             )
 
-        def quant_q(i):
-            quantize(q_codes[i][:], q_scales[i][:], q_bf[i][:].rearrange("p c j -> p (c j)"))
+        def copy_q(n, copy):
+            copy(
+                out=q_bf[n][:].rearrange("p (c i) j -> p c j i", i=RUN),
+                in_=q_raw[n][:].rearrange("p j (c i) -> p c j i", i=RUN),
+            )
+
+        def quant_q(n):
+            quantize(q_codes[n][:], q_scales[n][:], q_bf[n][:].rearrange("p c j -> p (c j)"))
 
         def copy_v(h):
-            g, a = divmod(h, 2)
+            g, a = divmod(h, SIDES)
             nc.vector.tensor_tensor(
-                out=v_bf[g][:, a].rearrange("p (c i) j -> p c j i", i=2),
-                in0=v_raw[g][:, a].rearrange("p j (c i) -> p c j i", i=2),
-                in1=t_sign[:].unsqueeze(1).unsqueeze(3).to_broadcast([P, E // 2, PACK, 2]),
+                out=v_bf[g][:, a].rearrange("s (c i) r -> s c r i", i=RUN),
+                in0=v_raw[g][:, a].rearrange("s r (c i) -> s c r i", i=RUN),
+                in1=t_sign[:].unsqueeze(1).unsqueeze(3).to_broadcast([P, E // RUN, PACK, RUN]),
                 op=ALU.mult,
             )
 
         def quant_v(g):
-            quantize(v_codes[g][:], v_scales[g][:], v_bf[g][:].rearrange("p h e j -> p (h e j)"))
+            quantize(v_codes[g][:], v_scales[g][:], v_bf[g][:].rearrange("s a e r -> s (a e r)"))
 
-        def scores(grp, z):
-            g, a, m = place(grp, 2 * z)
-            i = [n for n, (gg, lo, hi) in enumerate(Q_LOADS) if gg == g and lo <= m < hi][0]
-            q_cols = slice((m - Q_LOADS[i][1]) * QT, (m - Q_LOADS[i][1] + 1) * QT)
-            for r in range(PACK):
-                cols = slice(r * P, (r + 1) * P)
-                for a in range(2):
-                    rows = slice(a * ROWS, (a + 1) * ROWS)
+        def scores(grp):
+            for z in range(items[grp]):
+                g, a, m = place(grp, z)
+                n = [n for n, (pair, first, end) in enumerate(Q_LOADS) if pair == g and first <= m < end][0]
+                q_first = (m - Q_LOADS[n][1]) * QT
+                q_cols = slice(q_first, q_first + QT)
+                rows = slice(a * ROWS, (a + 1) * ROWS)
+                for r in range(PACK):
+                    k_cols = slice(r * P, (r + 1) * P)
                     nc.tensor.matmul_mx(
                         out=score[a][m % SCORE_BANKS][:, r, :],
-                        lhsT=k_codes[g][rows, cols].bitcast(FP8X4),
-                        lhsT_scale=k_scales[g][rows, cols],
-                        rhs=q_codes[i][rows, q_cols].bitcast(FP8X4),
-                        rhs_scale=q_scales[i][rows, q_cols],
+                        lhsT=k_codes[g][rows, k_cols].bitcast(FP8X4),
+                        lhsT_scale=k_scales[g][rows, k_cols],
+                        rhs=q_codes[n][rows, q_cols].bitcast(FP8X4),
+                        rhs_scale=q_scales[n][rows, q_cols],
                         start=True,
                         stop=True,
                     )
 
-        def cap(grp, z):
-            g, a, m = place(grp, z)
-            nc.scalar.activation(
-                out=th[grp][:, :, z * QT : (z + 1) * QT],
-                in_=score[a][m % SCORE_BANKS][:],
-                func=ACT.Tanh,
-                scale=1.0 / CAP,
-            )
-
-        def relu_scale(grp, r):
-            nc.vector.tensor_scalar(
-                out=root_w[grp][:, r, :],
-                in0=th[grp][:, r, :],
-                scalar1=0.0,
-                scalar2=t_root[:, r : r + 1],
-                op0=ALU.max,
-                op1=ALU.mult,
-            )
-
-        def square(grp, lo, hi, on_scalar):
-            src = root_w[grp][:, :, lo * QT : hi * QT].rearrange("p r (c i) -> p c r i", i=2)
-            dst = w_bf[grp][:, lo * QT : hi * QT, :].rearrange("p (c i) r -> p c r i", i=2)
-            if on_scalar:
-                nc.scalar.activation(out=dst, in_=src, func=ACT.Square)
-            else:
-                nc.vector.tensor_tensor(out=dst, in0=src, in1=src, op=ALU.mult)
-
-        def quant_w(grp, lo, hi):
-            cols = slice(lo * QT, hi * QT)
-            quantize(w_codes[grp][:, cols], w_scales[grp][:, cols], w_bf[grp][:, cols, :].rearrange("p c r -> p (c r)"))
-
-        def values(grp, lo, hi):
-            for z in range(lo, hi):
+        def cap(grp, *zs):
+            for z in zs:
                 g, a, m = place(grp, z)
-                cols = slice(z * QT, (z + 1) * QT)
+                nc.scalar.activation(
+                    out=capped[grp][:, :, z * QT : (z + 1) * QT],
+                    in_=score[a][m % SCORE_BANKS][:],
+                    func=ACT.Tanh,
+                    scale=1.0 / CAP,
+                )
+
+        def relu_scale(grp, *rs):
+            for r in rs:
+                nc.vector.tensor_scalar(
+                    out=root_w[grp][:, r, :],
+                    in0=capped[grp][:, r, :],
+                    scalar1=0.0,
+                    scalar2=t_root[:, r : r + 1],
+                    op0=ALU.max,
+                    op1=ALU.mult,
+                )
+
+        def square_views(grp, tile):
+            cols = slice(tile * SIDES * QT, (tile + 1) * SIDES * QT)
+            src = root_w[grp][:, :, cols].rearrange("s r (c i) -> s c r i", i=RUN)
+            dst = w_bf[grp][:, cols, :].rearrange("s (c i) r -> s c r i", i=RUN)
+            return src, dst
+
+        def square(grp, tile):
+            src, dst = square_views(grp, tile)
+            nc.scalar.activation(out=dst, in_=src, func=ACT.Square)
+
+        def square_on_vector(grp, tile):
+            src, dst = square_views(grp, tile)
+            nc.vector.tensor_tensor(out=dst, in0=src, in1=src, op=ALU.mult)
+
+        def quant_w(grp):
+            quantize(w_codes[grp][:], w_scales[grp][:], w_bf[grp][:].rearrange("s c r -> s (c r)"))
+
+        def values(grp):
+            for z in range(items[grp]):
+                g, a, m = place(grp, z)
+                w_cols = slice(z * QT, (z + 1) * QT)
                 v_cols = slice(a * E, (a + 1) * E)
                 nc.tensor.matmul_mx(
                     out=y_ps[grp % Y_BANKS][:, z, :],
-                    lhsT=w_codes[grp][:, cols].bitcast(FP8X4),
-                    lhsT_scale=w_scales[grp][:, cols],
+                    lhsT=w_codes[grp][:, w_cols].bitcast(FP8X4),
+                    lhsT_scale=w_scales[grp][:, w_cols],
                     rhs=v_codes[g][:, v_cols].bitcast(FP8X4),
                     rhs_scale=v_scales[g][:, v_cols],
                     start=True,
@@ -240,37 +226,178 @@ def tile_rows_a_relu2_cap_gate_kernel(tc, qT, kT, t, v, og, out):
 
         def den_add(grp):
             nc.vector.tensor_scalar(
-                out=den[grp][:], in0=y_ps[grp % Y_BANKS][:, : slots[grp], E - 1 : E], scalar1=1.0, scalar2=None, op0=ALU.add
+                out=den[grp][:],
+                in0=y_ps[grp % Y_BANKS][:, : items[grp], E - 1 : E],
+                scalar1=1.0,
+                scalar2=None,
+                op0=ALU.add,
             )
 
         def den_recip(grp):
-            nc.vector.reciprocal(out=rden[grp][:], in_=den[grp][:].rearrange("p a o -> p (a o)"))
+            nc.vector.reciprocal(out=rden[grp][:], in_=den[grp][:].rearrange("p z o -> p (z o)"))
 
-        def finish(grp, z):
-            g, a, m = place(grp, z)
-            nc.vector.scalar_tensor_tensor(
-                out=res[grp][:, z, :],
-                in0=y_ps[grp % Y_BANKS][:, z, :],
-                scalar=rden[grp][:, z : z + 1],
-                in1=gate_of(2 * g + a, m),
-                op0=ALU.mult,
-                op1=ALU.mult,
-            )
+        def gates(*ns):
+            for n in ns:
+                nc.scalar.activation(out=gate[n][:], in_=og_raw[n][:], func=ACT.Sigmoid)
 
-        def store(grp, lo, hi):
-            g, a, m = place(grp, lo)
+        def finish(grp, *zs):
+            for z in zs:
+                g, a, m = place(grp, z)
+                head = SIDES * g + a
+                n = [
+                    n
+                    for n, (h, h_end, first, end) in enumerate(OG_LOADS)
+                    if h <= head < h_end and first <= m < end
+                ][0]
+                h, h_end, first, end = OG_LOADS[n]
+                nc.vector.scalar_tensor_tensor(
+                    out=res[grp][:, z, :],
+                    in0=y_ps[grp % Y_BANKS][:, z, :],
+                    scalar=rden[grp][:, z : z + 1],
+                    in1=gate[n][:, (head - h) * (end - first) + m - first, :],
+                    op0=ALU.mult,
+                    op1=ALU.mult,
+                )
+
+        def store(grp, z_first, z_end):
+            g, a, m = place(grp, z_first)
+            head = SIDES * g + a
             nc.sync.dma_start(
-                out=out[2 * g + a : 2 * g + a + hi - lo, m * QT : (m + 1) * QT, :].rearrange("h p e -> p h e"),
-                in_=res[grp][:, lo:hi, :],
+                out=out[head : head + z_end - z_first, m * QT : (m + 1) * QT, :].rearrange("h p e -> p h e"),
+                in_=res[grp][:, z_first:z_end, :],
             )
 
-        steps = {
-            "lk": load_k, "lq": load_q, "lv": load_v, "lo": load_og, "lt": load_t, "half": make_half, "root": root, "sign": sign,
-            "sig": sigmoid, "ck": copy_k, "qk": quant_k, "cq": copy_q, "qq": quant_q, "cv": copy_v, "qv": quant_v,
-            "sc": scores, "cap": cap, "rs": relu_scale, "sq": square, "qw": quant_w, "val": values,
-            "da": den_add, "dr": den_recip, "fin": finish, "st": store,
-        }
         with tc.manual_schedule():
-            for word in ORDER:
-                parts = word.split(":")
-                steps[parts[0]](*[int(c) for c in parts[1]])
+            load_k(0)
+            load_q(0)
+            nc.sync.dma_start(out=t_sb[:], in_=t.rearrange("(s r) o -> s (r o)", r=PACK))
+            load_q(1)
+            load_q(2)
+            load_k(1)
+            load_q(3)
+            load_q(4)
+            load_v(0)
+            load_og(0)
+            load_og(1)
+            load_v(1)
+            for n in range(2, len(OG_LOADS)):
+                load_og(n)
+
+            nc.gpsimd.memset(zero[:], 0.0)
+            nc.scalar.activation(out=half[:], in_=zero[:], func=ACT.Sigmoid)
+
+            copy_k(0, 0, K_SPLIT, nc.vector.tensor_copy)
+            copy_k(0, K_SPLIT, P, nc.scalar.copy)
+            copy_q(0, nc.scalar.copy)
+            nc.scalar.activation(out=t_abs[:], in_=t_sb[:], func=ACT.Abs, scale=CAP * CAP)
+            nc.gpsimd.tensor_tensor(out=t_root[:], in0=t_abs[:], in1=half[:], op=ALU.pow)
+            quant_k(0, 0, 2)
+            nc.vector.tensor_scalar(
+                out=t_step[:], in0=t_sb[:], scalar1=0.0, scalar2=2.0, op0=ALU.is_ge, op1=ALU.mult
+            )
+            quant_q(0)
+            quant_k(0, 2, 4)
+            scores(0)
+            copy_q(1, nc.vector.tensor_copy)
+            nc.vector.tensor_scalar(out=t_sign[:], in0=t_step[:], scalar1=-1.0, scalar2=None, op0=ALU.add)
+            quant_q(1)
+            scores(1)
+            copy_q(2, nc.vector.tensor_copy)
+
+            cap(0, 0, 1)
+            cap(1, 0, 1)
+            quant_q(2)
+            scores(2)
+            relu_scale(0, 0, 1, 2, 3)
+            square(0, 0)
+            copy_k(1, 0, P // 2, nc.vector.tensor_copy)
+            relu_scale(1, 0, 1)
+            copy_k(1, P // 2, P, nc.vector.tensor_copy)
+            copy_q(3, nc.vector.tensor_copy)
+            relu_scale(1, 2, 3)
+            quant_q(3)
+            quant_k(1, 0, 4)
+
+            cap(2, 0, 1, 2, 3)
+            square(1, 0)
+            scores(3)
+            copy_q(4, nc.vector.tensor_copy)
+            copy_v(0)
+            relu_scale(2, 0)
+            quant_q(4)
+            quant_w(0)
+            relu_scale(2, 1, 2)
+            copy_v(1)
+            quant_w(1)
+            relu_scale(2, 3)
+            quant_v(0)
+
+            cap(3, 0, 1, 2, 3)
+            scores(4)
+            scores(5)
+            values(0)
+            values(1)
+            cap(4, 0, 1)
+            cap(5, 0)
+            square(2, 0)
+            cap(5, 1)
+            square(2, 1)
+            relu_scale(3, 0, 1)
+            copy_v(2)
+            copy_v(3)
+            relu_scale(4, 0, 1, 2)
+            relu_scale(3, 2)
+            den_add(0)
+            relu_scale(3, 3)
+            den_add(1)
+            relu_scale(4, 3)
+            den_recip(0)
+            quant_v(1)
+            relu_scale(5, 0, 1, 2)
+            quant_w(2)
+            values(2)
+            den_recip(1)
+
+            square_on_vector(4, 0)
+            gates(0, 1)
+            square(3, 0)
+            square(3, 1)
+            finish(0, 0, 1)
+            store(0, 0, 2)
+            den_add(2)
+            quant_w(4)
+            values(4)
+            den_recip(2)
+            relu_scale(5, 3)
+            gates(2, 3)
+            square(5, 0)
+            quant_w(3)
+            values(3)
+
+            finish(1, 0, 1)
+            store(1, 0, 2)
+            finish(2, 0)
+            den_add(4)
+            finish(2, 1)
+            store(2, 0, 2)
+            finish(2, 2)
+            den_recip(4)
+            finish(2, 3)
+            store(2, 2, 4)
+            den_add(3)
+            quant_w(5)
+            values(5)
+            den_recip(3)
+            gates(4, 5, 6, 7)
+            finish(4, 0, 1)
+            store(4, 0, 2)
+            finish(3, 0, 1)
+            store(3, 0, 2)
+            den_add(5)
+            finish(3, 2)
+            den_recip(5)
+            finish(3, 3)
+            store(3, 2, 4)
+            for z in range(items[5]):
+                finish(5, z)
+                store(5, z, z + 1)

from contextlib import ExitStack

import concourse.mybir as mybir

H, D, NQ, N, E = 4, 256, 512, 512, 128
CAP = 2.0
FLOPS = 2 * H * NQ * N * (D + E)

F32 = mybir.dt.float32
BF16 = mybir.dt.bfloat16
U32 = mybir.dt.uint32
U8 = mybir.dt.uint8
FP8X4 = mybir.dt.float8_e4m3fn_x4
ALU = mybir.AluOpType
ACT = mybir.ActivationFunctionType

P = 128
PACK = 4
SIDES = 2
PAIRS = H // SIDES
ROWS = P // SIDES
QT = 128
RUN = 2
SCORE_BANKS = 2
Y_BANKS = 4

GROUPS = [(0, 0, 1), (0, 1, 2), (0, 2, 4), (1, 0, 2), (1, 2, 3), (1, 3, 4)]
Q_LOADS = [(0, 0, 1), (0, 1, 2), (0, 2, 4), (1, 0, 2), (1, 2, 4)]
OG_LOADS = [
    (0, 2, 0, 1), (0, 2, 1, 2), (0, 1, 2, 4), (1, 2, 2, 4),
    (2, 4, 2, 3), (2, 3, 0, 2), (3, 4, 0, 2), (2, 4, 3, 4),
]
K_SPLIT = 88


def tile_rows_a_relu2_cap_gate_kernel(tc, qT, kT, t, v, og, out):
    nc = tc.nc
    q_rows = qT.rearrange("h (p j) n -> (h p) j n", j=PACK)
    k_rows = kT.rearrange("h (p j) n -> (h p) j n", j=PACK)

    with ExitStack() as ctx:
        sb = ctx.enter_context(tc.tile_pool(name="sb", bufs=1))
        ps = ctx.enter_context(tc.psum_pool(name="ps", bufs=1))

        def tiles(name, shapes, dtype):
            return [sb.tile(shape, dtype, name=name + str(n), align_bytes=64) for n, shape in enumerate(shapes)]

        score = [
            [ps.tile([P, PACK, QT], F32, name="score%d_%d" % (a, b)) for b in range(SCORE_BANKS)]
            for a in range(SIDES)
        ]
        y_ps = [ps.tile([P, 2 * SIDES, E], F32, name="y%d" % b) for b in range(Y_BANKS)]

        t_sb = sb.tile([P, PACK], F32, name="t_sb")
        t_step = sb.tile([P, PACK], F32, name="t_step")
        t_sign = sb.tile([P, PACK], F32, name="t_sign")
        t_abs = sb.tile([P, PACK], F32, name="t_abs")
        zero = sb.tile([P, PACK], F32, name="zero")
        half = sb.tile([P, PACK], F32, name="half")
        t_root = sb.tile([P, PACK], F32, name="t_root")

        k_raw = tiles("k_raw", [[P, PACK, N]] * PAIRS, F32)
        k_bf = tiles("k_bf", [[P, PACK, P, PACK]] * PAIRS, BF16)
        k_codes = tiles("k_codes", [[P, N]] * PAIRS, U32)
        k_scales = tiles("k_scales", [[P, N]] * PAIRS, U8)

        q_width = [(end - first) * QT for g, first, end in Q_LOADS]
        q_raw = tiles("q_raw", [[P, PACK, width] for width in q_width], F32)
        q_bf = tiles("q_bf", [[P, width, PACK] for width in q_width], BF16)
        q_codes = tiles("q_codes", [[P, width] for width in q_width], U32)
        q_scales = tiles("q_scales", [[P, width] for width in q_width], U8)

        v_raw = tiles("v_raw", [[P, SIDES, PACK, E]] * PAIRS, F32)
        v_bf = tiles("v_bf", [[P, SIDES, E, PACK]] * PAIRS, BF16)
        v_codes = tiles("v_codes", [[P, SIDES * E]] * PAIRS, U32)
        v_scales = tiles("v_scales", [[P, SIDES * E]] * PAIRS, U8)

        og_shapes = [[P, (h_end - h) * (end - first), E] for h, h_end, first, end in OG_LOADS]
        og_raw = tiles("og_raw", og_shapes, F32)
        gate = tiles("gate", og_shapes, F32)

        items = [SIDES * (end - first) for g, first, end in GROUPS]
        capped = tiles("capped", [[P, PACK, count * QT] for count in items], F32)
        root_w = tiles("root_w", [[P, PACK, count * QT] for count in items], F32)
        w_bf = tiles("w_bf", [[P, count * QT, PACK] for count in items], BF16)
        w_codes = tiles("w_codes", [[P, count * QT] for count in items], U32)
        w_scales = tiles("w_scales", [[P, count * QT] for count in items], U8)
        den = tiles("den", [[P, count, 1] for count in items], F32)
        rden = tiles("rden", [[P, count] for count in items], F32)
        res = tiles("res", [[P, count, E] for count in items], F32)

        def place(grp, z):
            g, first, end = GROUPS[grp]
            return g, z % SIDES, first + z // SIDES

        def load_k(g):
            nc.sync.dma_start(out=k_raw[g][:], in_=k_rows[g * P : (g + 1) * P])

        def load_q(n):
            g, first, end = Q_LOADS[n]
            nc.sync.dma_start(out=q_raw[n][:], in_=q_rows[g * P : (g + 1) * P, :, first * QT : end * QT])

        def load_v(g):
            nc.sync.dma_start(
                out=v_raw[g][:].rearrange("s a r e -> s a (r e)"),
                in_=v[SIDES * g : SIDES * (g + 1)].rearrange("a (s r) e -> s a (r e)", r=PACK),
            )

        def load_og(n):
            h, h_end, first, end = OG_LOADS[n]
            if h_end - h == 1:
                src = og[h, first * QT : end * QT, :].rearrange("(m p) e -> p m e", p=P)
            else:
                src = og[h:h_end, first * QT : end * QT, :].rearrange("h p e -> p h e")
            nc.sync.dma_start(out=og_raw[n][:], in_=src)

        def quantize(codes, scales, src):
            nc.vector.quantize_mx(out=codes.bitcast(FP8X4), scales=scales, in_=src)

        def copy_k(g, s_first, s_end, copy):
            copy(
                out=k_bf[g][:, :, s_first:s_end, :].rearrange("p r s j -> p s j r"),
                in_=k_raw[g][:, :, s_first * PACK : s_end * PACK].rearrange("p j (s r) -> p s j r", r=PACK),
            )

        def quant_k(g, r_first, r_end):
            cols = slice(r_first * P, r_end * P)
            quantize(
                k_codes[g][:, cols],
                k_scales[g][:, cols],
                k_bf[g][:, r_first:r_end].rearrange("p r s j -> p (r s j)"),
            )

        def copy_q(n, copy):
            copy(
                out=q_bf[n][:].rearrange("p (c i) j -> p c j i", i=RUN),
                in_=q_raw[n][:].rearrange("p j (c i) -> p c j i", i=RUN),
            )

        def quant_q(n):
            quantize(q_codes[n][:], q_scales[n][:], q_bf[n][:].rearrange("p c j -> p (c j)"))

        def copy_v(h):
            g, a = divmod(h, SIDES)
            nc.vector.tensor_tensor(
                out=v_bf[g][:, a].rearrange("s (c i) r -> s c r i", i=RUN),
                in0=v_raw[g][:, a].rearrange("s r (c i) -> s c r i", i=RUN),
                in1=t_sign[:].unsqueeze(1).unsqueeze(3).to_broadcast([P, E // RUN, PACK, RUN]),
                op=ALU.mult,
            )

        def quant_v(g):
            quantize(v_codes[g][:], v_scales[g][:], v_bf[g][:].rearrange("s a e r -> s (a e r)"))

        def scores(grp):
            for z in range(items[grp]):
                g, a, m = place(grp, z)
                n = [n for n, (pair, first, end) in enumerate(Q_LOADS) if pair == g and first <= m < end][0]
                q_first = (m - Q_LOADS[n][1]) * QT
                q_cols = slice(q_first, q_first + QT)
                rows = slice(a * ROWS, (a + 1) * ROWS)
                for r in range(PACK):
                    k_cols = slice(r * P, (r + 1) * P)
                    nc.tensor.matmul_mx(
                        out=score[a][m % SCORE_BANKS][:, r, :],
                        lhsT=k_codes[g][rows, k_cols].bitcast(FP8X4),
                        lhsT_scale=k_scales[g][rows, k_cols],
                        rhs=q_codes[n][rows, q_cols].bitcast(FP8X4),
                        rhs_scale=q_scales[n][rows, q_cols],
                        start=True,
                        stop=True,
                    )

        def cap(grp, *zs):
            for z in zs:
                g, a, m = place(grp, z)
                nc.scalar.activation(
                    out=capped[grp][:, :, z * QT : (z + 1) * QT],
                    in_=score[a][m % SCORE_BANKS][:],
                    func=ACT.Tanh,
                    scale=1.0 / CAP,
                )

        def relu_scale(grp, *rs):
            for r in rs:
                nc.vector.tensor_scalar(
                    out=root_w[grp][:, r, :],
                    in0=capped[grp][:, r, :],
                    scalar1=0.0,
                    scalar2=t_root[:, r : r + 1],
                    op0=ALU.max,
                    op1=ALU.mult,
                )

        def square_views(grp, tile):
            cols = slice(tile * SIDES * QT, (tile + 1) * SIDES * QT)
            src = root_w[grp][:, :, cols].rearrange("s r (c i) -> s c r i", i=RUN)
            dst = w_bf[grp][:, cols, :].rearrange("s (c i) r -> s c r i", i=RUN)
            return src, dst

        def square(grp, tile):
            src, dst = square_views(grp, tile)
            nc.scalar.activation(out=dst, in_=src, func=ACT.Square)

        def square_on_vector(grp, tile):
            src, dst = square_views(grp, tile)
            nc.vector.tensor_tensor(out=dst, in0=src, in1=src, op=ALU.mult)

        def quant_w(grp):
            quantize(w_codes[grp][:], w_scales[grp][:], w_bf[grp][:].rearrange("s c r -> s (c r)"))

        def values(grp):
            for z in range(items[grp]):
                g, a, m = place(grp, z)
                w_cols = slice(z * QT, (z + 1) * QT)
                v_cols = slice(a * E, (a + 1) * E)
                nc.tensor.matmul_mx(
                    out=y_ps[grp % Y_BANKS][:, z, :],
                    lhsT=w_codes[grp][:, w_cols].bitcast(FP8X4),
                    lhsT_scale=w_scales[grp][:, w_cols],
                    rhs=v_codes[g][:, v_cols].bitcast(FP8X4),
                    rhs_scale=v_scales[g][:, v_cols],
                    start=True,
                    stop=True,
                )

        def den_add(grp):
            nc.vector.tensor_scalar(
                out=den[grp][:],
                in0=y_ps[grp % Y_BANKS][:, : items[grp], E - 1 : E],
                scalar1=1.0,
                scalar2=None,
                op0=ALU.add,
            )

        def den_recip(grp):
            nc.vector.reciprocal(out=rden[grp][:], in_=den[grp][:].rearrange("p z o -> p (z o)"))

        def gates(*ns):
            for n in ns:
                nc.scalar.activation(out=gate[n][:], in_=og_raw[n][:], func=ACT.Sigmoid)

        def finish(grp, *zs):
            for z in zs:
                g, a, m = place(grp, z)
                head = SIDES * g + a
                n = [
                    n
                    for n, (h, h_end, first, end) in enumerate(OG_LOADS)
                    if h <= head < h_end and first <= m < end
                ][0]
                h, h_end, first, end = OG_LOADS[n]
                nc.vector.scalar_tensor_tensor(
                    out=res[grp][:, z, :],
                    in0=y_ps[grp % Y_BANKS][:, z, :],
                    scalar=rden[grp][:, z : z + 1],
                    in1=gate[n][:, (head - h) * (end - first) + m - first, :],
                    op0=ALU.mult,
                    op1=ALU.mult,
                )

        def store(grp, z_first, z_end):
            g, a, m = place(grp, z_first)
            head = SIDES * g + a
            nc.sync.dma_start(
                out=out[head : head + z_end - z_first, m * QT : (m + 1) * QT, :].rearrange("h p e -> p h e"),
                in_=res[grp][:, z_first:z_end, :],
            )

        with tc.manual_schedule():
            load_k(0)
            load_q(0)
            nc.sync.dma_start(out=t_sb[:], in_=t.rearrange("(s r) o -> s (r o)", r=PACK))
            load_q(1)
            load_q(2)
            load_k(1)
            load_q(3)
            load_q(4)
            load_v(0)
            load_og(0)
            load_og(1)
            load_v(1)
            for n in range(2, len(OG_LOADS)):
                load_og(n)

            nc.gpsimd.memset(zero[:], 0.0)
            nc.scalar.activation(out=half[:], in_=zero[:], func=ACT.Sigmoid)

            copy_k(0, 0, K_SPLIT, nc.vector.tensor_copy)
            copy_k(0, K_SPLIT, P, nc.scalar.copy)
            copy_q(0, nc.scalar.copy)
            nc.scalar.activation(out=t_abs[:], in_=t_sb[:], func=ACT.Abs, scale=CAP * CAP)
            nc.gpsimd.tensor_tensor(out=t_root[:], in0=t_abs[:], in1=half[:], op=ALU.pow)
            quant_k(0, 0, 2)
            nc.vector.tensor_scalar(
                out=t_step[:], in0=t_sb[:], scalar1=0.0, scalar2=2.0, op0=ALU.is_ge, op1=ALU.mult
            )
            quant_q(0)
            quant_k(0, 2, 4)
            scores(0)
            copy_q(1, nc.vector.tensor_copy)
            nc.vector.tensor_scalar(out=t_sign[:], in0=t_step[:], scalar1=-1.0, scalar2=None, op0=ALU.add)
            quant_q(1)
            scores(1)
            copy_q(2, nc.vector.tensor_copy)

            cap(0, 0, 1)
            cap(1, 0, 1)
            quant_q(2)
            scores(2)
            relu_scale(0, 0, 1, 2, 3)
            square(0, 0)
            copy_k(1, 0, P // 2, nc.vector.tensor_copy)
            relu_scale(1, 0, 1)
            copy_k(1, P // 2, P, nc.vector.tensor_copy)
            copy_q(3, nc.vector.tensor_copy)
            relu_scale(1, 2, 3)
            quant_q(3)
            quant_k(1, 0, 4)

            cap(2, 0, 1, 2, 3)
            square(1, 0)
            scores(3)
            copy_q(4, nc.vector.tensor_copy)
            copy_v(0)
            relu_scale(2, 0)
            quant_q(4)
            quant_w(0)
            relu_scale(2, 1, 2)
            copy_v(1)
            quant_w(1)
            relu_scale(2, 3)
            quant_v(0)

            cap(3, 0, 1, 2, 3)
            scores(4)
            scores(5)
            values(0)
            values(1)
            cap(4, 0, 1)
            cap(5, 0)
            square(2, 0)
            cap(5, 1)
            square(2, 1)
            relu_scale(3, 0, 1)
            copy_v(2)
            copy_v(3)
            relu_scale(4, 0, 1, 2)
            relu_scale(3, 2)
            den_add(0)
            relu_scale(3, 3)
            den_add(1)
            relu_scale(4, 3)
            den_recip(0)
            quant_v(1)
            relu_scale(5, 0, 1, 2)
            quant_w(2)
            values(2)
            den_recip(1)

            square_on_vector(4, 0)
            gates(0, 1)
            square(3, 0)
            square(3, 1)
            finish(0, 0, 1)
            store(0, 0, 2)
            den_add(2)
            quant_w(4)
            values(4)
            den_recip(2)
            relu_scale(5, 3)
            gates(2, 3)
            square(5, 0)
            quant_w(3)
            values(3)

            finish(1, 0, 1)
            store(1, 0, 2)
            finish(2, 0)
            den_add(4)
            finish(2, 1)
            store(2, 0, 2)
            finish(2, 2)
            den_recip(4)
            finish(2, 3)
            store(2, 2, 4)
            den_add(3)
            quant_w(5)
            values(5)
            den_recip(3)
            gates(4, 5, 6, 7)
            finish(4, 0, 1)
            store(4, 0, 2)
            finish(3, 0, 1)
            store(3, 0, 2)
            den_add(5)
            finish(3, 2)
            den_recip(5)
            finish(3, 3)
            store(3, 2, 4)
            for z in range(items[5]):
                finish(5, z)
                store(5, z, z + 1)
